import numpy as np, ml_dtypes
CORES = [2,10,50,58,66,74,122]
N = 7
import mx_ref
NC, KT, ROOT = 128, 3, 6
BF = ml_dtypes.bfloat16
def setup_inputs(rng):
    def f(*shape):
        return mx_ref.flush((rng.standard_normal(shape, dtype=np.float32) * np.exp2(rng.integers(-2, 3, shape[:-1] + (1,)))).astype(BF))
    return {"w": f(N, 128, KT * 512), "x": f(N, 128, N * KT * 4 * NC)}
def setup_inputs_blocks(rng):
    d = setup_inputs(rng)
    for k in ("w", "x"): d[k] = mx_ref.spread(d[k], rng, 1)
    return d
def setup_inputs_wide(rng):
    d = setup_inputs(rng)
    for k in ("w", "x"): d[k] = mx_ref.flush((d[k].astype(np.float32) * np.exp2(rng.integers(-8, 9, (N, 1, 1))).astype(np.float32)).astype(BF))
    return d
def setup_inputs_zeros(rng):
    d = setup_inputs(rng); v = d["x"].reshape(N, 128, -1, 4).copy()
    v[np.broadcast_to((rng.random((N, 1, v.shape[2], 1)) < 0.33), v.shape)] = 0
    d["x"] = v.reshape(d["x"].shape)
    return d
def reference(w, x):
    y = np.zeros((N, 128, NC), np.float32)
    for r in range(N):
        for t in range(KT):
            p = mx_ref.matmul(mx_ref.quantize(w[r][:, 512 * t:512 * t + 512]), mx_ref.quantize(x[ROOT][:, 4 * NC * (KT * r + t):4 * NC * (KT * r + t) + 4 * NC]))
            y[r] = p if t == 0 else y[r] + p
    return {"y": y}

from concourse.mybir import dt

N = 7
KT = 3
NC = 128
CW = KT * NC
XE = 4 * CW
WINDOW = 3

SCRATCH = {
    "xb": ("sbuf", [128, N * XE], "bfloat16"),
    "wb": ("sbuf", [128, XE], "bfloat16"),
    "xq": ("sbuf", [128, N * CW], "float8_e4m3fn_x4"),
    "xs": ("sbuf", [128, N * CW], "uint8"),
    "wq": ("sbuf", [128, CW], "float8_e4m3fn_x4"),
    "ws": ("sbuf", [128, CW], "uint8"),
    "lq": ("sbuf", [128, CW], "float8_e4m3fn_x4"),
    "ls": ("sbuf", [128, CW], "uint8"),
    "yb": ("sbuf", [128, NC], "float32"),
    "ps": ("psum", [128, 512], "float32"),
}
SEMAPHORES = (["ld%d" % i for i in range(N + 1)] + ["q%d" % i for i in range(N + 1)]
              + ["hs", "hc", "arr", "sent", "mm", "cp", "st"])


def _count(mask):
    return bin(mask).count("1")


def _plan(T, topo):
    root = T.cores[T.root]
    pool = [c for c in range(topo.CHIPS * topo.CORES_PER_CHIP)
            if c != root and topo.chip(c) == topo.chip(root) and topo.die(c) == topo.die(root)
            and T.rank_of(c) is None]
    via = {}
    for r, dst in enumerate(T.cores):
        if r == T.root:
            continue
        via[r] = None
        if topo.same_plane(topo.chip(root), topo.chip(dst)):
            free = [c for c in pool if c not in via.values() and topo.may_write(c, dst)]
            if free:
                via[r] = free[0]
    order = [r for r in via if via[r] is not None] + [r for r in via if via[r] is None]
    return root, via, order


def _send(g, T, topo, dst, mask, src_q, src_s, sem_s, sem_q):
    rid, pid, _ = topo.addr(dst)
    g.remote_dma(T.ls[:, :], src_s, sem_s, T.sem.sent, pid, rid, mask)
    g.remote_dma(T.lq[:, :].bitcast(dt.uint8), src_q.bitcast(dt.uint8), sem_q, T.sem.sent, pid, rid, mask)
    return 2 * _count(mask)


def _finish(g, T, xq, xs, base):
    for t in range(KT):
        mm = g.tensor.matmul_mx(T.ps[:, 0:NC], T.wq[:, NC * t:NC * t + NC], T.ws[:, NC * t:NC * t + NC],
                                xq[:, base + NC * t:base + NC * t + NC], xs[:, base + NC * t:base + NC * t + NC],
                                t == 0, t == KT - 1)
    mm.then_inc(T.sem.mm, 1)
    g.vector.wait_ge(T.sem.mm, 1)
    g.vector.tensor_copy(T.yb[:, :], T.ps[:, 0:NC]).then_inc(T.sem.cp, 1)
    g.sync.wait_ge(T.sem.cp, 1)
    g.sync.dma_start(T.y[:, :], T.yb[:, :]).then_inc(T.sem.st, 16)
    g.sync.wait_ge(T.sem.st, 16)


def rank_program(g, core, T, topo):
    root, via, order = _plan(T, topo)
    rank = T.rank_of(core)

    if rank is None:
        mine = [r for r in order if via[r] == core]
        if not mine:
            return
        dst = T.cores[mine[0]]
        n_in = _count(topo.mask(root, core) & ~topo.mask(root, dst))
        out = topo.mask(core, dst)
        rid, pid, _ = topo.addr(dst)
        g.wait_ge(T.sem.hs, n_in)
        g.remote_dma(T.ls[:, :], T.ls[:, :], T.sem.arr, T.sem.sent, pid, rid, out)
        g.wait_ge(T.sem.hc, n_in)
        g.remote_dma(T.lq[:, :].bitcast(dt.uint8), T.lq[:, :].bitcast(dt.uint8), T.sem.arr, T.sem.sent, pid, rid, out)
        g.wait_ge(T.sem.sent, 2 * _count(out))
        return

    if core != root:
        g.sync.dma_start(T.wb[:, :], T.w[:, :]).then_inc(T.sem.ld0, 16)
        g.vector.wait_ge(T.sem.ld0, 16)
        g.vector.quantize_mx(T.wq[:, :], T.ws[:, :], T.wb[:, :]).then_inc(T.sem.q0, 1)
        sender = via[rank] if via[rank] is not None else root
        g.tensor.wait_ge(T.sem.q0, 1)
        g.tensor.wait_ge(T.sem.arr, 2 * _count(topo.mask(sender, core)))
        _finish(g, T, T.lq, T.ls, 0)
        return

    items = order + ["w", T.root]
    queues = [g.sync, g.scalar]
    for i, it in enumerate(items):
        qu = queues[i % 2]
        if i >= WINDOW:
            qu.wait_ge(T.sem["ld%d" % (i - WINDOW)], 16)
        if it == "w":
            qu.dma_start(T.wb[:, :], T.w[:, :]).then_inc(T.sem["ld%d" % i], 16)
        else:
            qu.dma_start(T.xb[:, XE * it:XE * it + XE], T.x[:, XE * it:XE * it + XE]).then_inc(T.sem["ld%d" % i], 16)
    for i, it in enumerate(items):
        g.vector.wait_ge(T.sem["ld%d" % i], 16)
        if it == "w":
            g.vector.quantize_mx(T.wq[:, :], T.ws[:, :], T.wb[:, :]).then_inc(T.sem["q%d" % i], 1)
        else:
            g.vector.quantize_mx(T.xq[:, CW * it:CW * it + CW], T.xs[:, CW * it:CW * it + CW],
                                 T.xb[:, XE * it:XE * it + XE]).then_inc(T.sem["q%d" % i], 1)
    total = 0
    for i, r in enumerate(order):
        dst = T.cores[r]
        g.wait_ge(T.sem["q%d" % i], 1)
        sq, ss = T.xq[:, CW * r:CW * r + CW], T.xs[:, CW * r:CW * r + CW]
        if via[r] is None:
            total += _send(g, T, topo, dst, topo.mask(root, dst), sq, ss, T.sem.arr, T.sem.arr)
        else:
            stay = topo.mask(root, via[r]) & ~topo.mask(root, dst)
            total += _send(g, T, topo, via[r], stay, sq, ss, T.sem.hs, T.sem.hc)
    g.tensor.wait_ge(T.sem["q%d" % (len(items) - 2)], 1)
    g.tensor.wait_ge(T.sem["q%d" % (len(items) - 1)], 1)
    _finish(g, T, T.xq, T.xs, CW * T.root)
    g.wait_ge(T.sem.sent, total)
